import numpy as np
import ml_dtypes


def mxq(x, axis, fmt="e4m3"):
    dtype, down = {"e4m3": (ml_dtypes.float8_e4m3fn, 7), "e5m2": (ml_dtypes.float8_e5m2, 14)}[fmt]
    v = np.moveaxis(np.asarray(x, np.float32).astype(ml_dtypes.bfloat16).astype(np.float64), axis, -1)
    blocks = v.reshape(v.shape[:-1] + (-1, 32))
    amax = np.abs(blocks).max(-1, keepdims=True)
    byte = np.maximum(np.where(amax > 0, np.frexp(amax)[1] - 1 + 127, 0) - down, 1)
    scale = np.exp2(byte - 127.0)
    codes = (blocks / scale).astype(np.float32).astype(dtype).astype(np.float64)
    return np.moveaxis((codes * scale).reshape(v.shape), -1, axis)


WIDE = False


def mx_kscale(k):
    if not WIDE:
        return np.ones(k)
    levels = np.array([10, -10, 5, -5, 0])
    if k % 512:
        return np.exp2(np.random.permutation(np.resize(levels, k // 32))).repeat(32)
    a = np.empty((k // 512, 16))
    for p in range(k // 512):
        a[p, :8] = np.random.permutation(np.resize(levels, 8))
        for g in range(8):
            far = levels[np.abs(levels - a[p, g]) >= 10]
            a[p, g + 8] = far[np.random.randint(len(far))]
    return np.exp2(a.ravel()).repeat(32)


def f64(x):
    return np.asarray(x).astype(np.float64)


def striped8(idx):
    return np.concatenate([v.reshape(-1, 16).T for v in idx]).astype(np.uint16)


def unstriped8(offs):
    return np.stack([offs[16 * g:16 * g + 16].T.reshape(-1) for g in range(8)]).astype(np.int64)


E2M1 = np.array([0.0, 0.5, 1.0, 1.5, 2.0, 3.0, 4.0, 6.0, -0.0, -0.5, -1.0, -1.5, -2.0, -3.0, -4.0, -6.0])


def pack_weight(w, fmt):
    k, n = w.shape
    w = f64(np.asarray(w, np.float32).astype(ml_dtypes.bfloat16)).reshape(k // 32, 32, n)
    amax = np.abs(w).max(1)
    if fmt == "e4m3":
        byte = np.frexp(amax)[1] - 1 + 127 - 7
    else:
        mant, ex = np.frexp(amax / 6.0)
        byte = np.where(mant > 0.5, ex, ex - 1) + 127
    byte = np.clip(np.where(amax > 0, byte, 1), 1, 254)
    scaled = (w * np.exp2(127.0 - byte)[:, None, :]).reshape(k, n).astype(np.float32)
    by_word = np.ascontiguousarray(scaled.reshape(k // 512, 128, 4, n).transpose(0, 1, 3, 2))
    if fmt == "e4m3":
        words = by_word.astype(ml_dtypes.float8_e4m3fn).view(np.uint8)
    else:
        c = by_word.astype(ml_dtypes.float4_e2m1fn).view(np.uint8) & 0xF
        words = (c[..., 0::2] | (c[..., 1::2] << 4)).reshape(k // 512, 128, 2 * n)
    return np.ascontiguousarray(words), np.ascontiguousarray(byte.astype(np.uint8).reshape(k // 512, 16, n))


def unpack_weight(words, scales, fmt):
    g, _, n = scales.shape
    words = np.ascontiguousarray(words).reshape(g, 128, n, -1)
    if fmt == "e4m3":
        vals = words.view(ml_dtypes.float8_e4m3fn).astype(np.float64)
    else:
        nib = np.empty((g, 128, n, 4), np.uint8)
        nib[..., 0::2] = words & 0xF
        nib[..., 1::2] = words >> 4
        vals = E2M1[nib]
    vals = vals * np.repeat(np.exp2(scales.astype(np.float64) - 127.0), 8, axis=1)[..., None]
    return vals.transpose(0, 1, 3, 2).reshape(g * 512, n)


def silu(v):
    return v / (1.0 + np.exp(-np.maximum(v, -700.0)))


K, M, T, S = 512, 1024, 1024, 512


def setup_inputs():
    n = np.random.standard_normal
    s = mx_kscale(K)[:, None]
    p_w4 = pack_weight(n((K, M)) / np.sqrt(K) / s, "e2m1")
    return {
        "xT": (n((K, T)) * s).astype(np.float32),
        "w4_words": p_w4[0],
        "w4_scales": p_w4[1],
        "w8": (n((K, M)) / np.sqrt(K) / s).astype(np.float32),
        "wgt": np.repeat(np.random.uniform(0.5, 2.0, (8, S)), 16, axis=0).astype(np.float32),
        "offs": striped8(np.stack([np.random.permutation(T)[:S] for _ in range(8)])),
    }


def reference(xT, w4_words, w4_scales, w8, wgt, offs):
    idx = unstriped8(offs)
    group = np.arange(K) % 512 // 64
    xg = f64(wgt)[np.arange(K) // 4 % 128] * f64(xT)[np.arange(K)[:, None], idx[group]]
    xT_ = mxq(xg, 0, "e4m3")
    w4_ = unpack_weight(w4_words, w4_scales, "e2m1")
    w8_ = mxq(f64(w8), 0, "e4m3")
    y = xT_.T @ w4_
    u = xT_.T @ w8_
    y = silu(y) * u
    return y

@@ -1,0 +1,179 @@
+from contextlib import ExitStack
+
+import concourse.mybir as mybir
+
+K, M, T, S = 512, 1024, 1024, 512
+FLOPS = 2 * 2 * K * M * S
+
+F32 = mybir.dt.float32
+BF16 = mybir.dt.bfloat16
+I32 = mybir.dt.int32
+U32 = mybir.dt.uint32
+U16 = mybir.dt.uint16
+U8 = mybir.dt.uint8
+FP8X4 = mybir.dt.float8_e4m3fn_x4
+FP4X4 = mybir.dt.float4_e2m1fn_x4
+MULT = mybir.AluOpType.mult
+ADD = mybir.AluOpType.add
+SILU = mybir.ActivationFunctionType.Silu
+
+P = 128
+PACK = 4
+J_TILE = 128
+N_GATE = 512
+N_UP = 256
+LIST_ROWS = 16
+X_ON = ["S","S","S","V"]
+W_ON = ["V","V","V","V","S","S","S","S"]
+
+
+def tile_list_hglu_tm_none_kernel(tc, xT, w4_words, w4_scales, w8, wgt, offs, out):
+    nc = tc.nc
+    j_tiles = S // J_TILE
+    chunks = M // N_UP
+
+    def interleave(engine, dst, src):
+        d = dst.rearrange("p (c i t) -> p c t i", i=4, t=PACK)
+        s = src.rearrange("p t (c i) -> p c t i", i=4)
+        if engine == "S":
+            nc.scalar.copy(out=d, in_=s)
+        elif engine == "V":
+            nc.vector.tensor_copy(out=d, in_=s)
+        else:
+            nc.gpsimd.tensor_scalar(out=d, in0=s, scalar1=1.0, scalar2=0.0, op0=MULT, op1=ADD)
+
+    with ExitStack() as ctx:
+        keep = ctx.enter_context(tc.tile_pool(name="keep", bufs=1))
+        psum = ctx.enter_context(tc.psum_pool(name="psum", bufs=4))
+
+        offsets = keep.tile([P, S // LIST_ROWS], U16, name="offsets")
+        gate_scales = keep.tile([P, M], U8, name="gate_scales", align_bytes=64)
+        nc.vector.memset(gate_scales[:].bitcast(I32), 0)
+
+        weights = keep.tile([P, S], F32, name="weights")
+        planes = [keep.tile([P, T], F32, name=f"plane{t}") for t in range(PACK)]
+        gate_words = keep.tile([P, 2 * M], U8, name="gate_words", align_bytes=64)
+        w_raw = [keep.tile([P, PACK, N_UP], F32, name=f"w_raw{c}") for c in range(chunks)]
+        x_rows = xT.rearrange("(p t) n -> p t n", t=PACK)
+        w_rows = w8.rearrange("(p t) n -> p t n", t=PACK)
+
+        def ld(name):
+            if name == "offs":
+                nc.sync.dma_start(offsets[:], offs)
+            elif name == "wgt":
+                nc.sync.dma_start(out=weights[:], in_=wgt)
+            elif name == "w4":
+                nc.sync.dma_start(out=gate_words[:].bitcast(I32), in_=w4_words[0].bitcast(I32))
+            elif name == "sc":
+                for q in range(4):
+                    nc.sync.dma_start(out=gate_scales[32 * q : 32 * q + 4, :].bitcast(I32), in_=w4_scales[0, 4 * q : 4 * q + 4, :].bitcast(I32))
+            elif name[0] == "x":
+                t = int(name[1])
+                nc.sync.dma_start(out=planes[t][:], in_=x_rows[:, t, :])
+            else:
+                c = int(name[1])
+                nc.sync.dma_start(out=w_raw[c][:], in_=w_rows[:, :, c * N_UP : (c + 1) * N_UP])
+
+        for name in ["offs","wgt","x0","sc","x1","x2","x3","w4","u0","u1","u2","u3"]:
+            ld(name)
+
+        G = 512
+        groups = S // G
+        picked = [keep.tile([P, PACK, G], F32, name=f"picked{h}") for h in range(groups)]
+        x_bf = [keep.tile([P, PACK * J_TILE], BF16, name=f"x_bf{j}", align_bytes=64) for j in range(j_tiles)]
+        x_codes = [keep.tile([P, J_TILE], U32, name=f"x_codes{j}", align_bytes=64) for j in range(j_tiles)]
+        x_scales = [keep.tile([P, J_TILE], U8, name=f"x_scales{j}", align_bytes=64) for j in range(j_tiles)]
+        w_bf = [keep.tile([P, PACK * N_UP], BF16, name=f"w_bf{c}", align_bytes=64) for c in range(chunks)]
+        w_codes = [keep.tile([P, N_UP], U32, name=f"w_codes{c}", align_bytes=64) for c in range(chunks)]
+        w_scales = [keep.tile([P, N_UP], U8, name=f"w_scales{c}", align_bytes=64) for c in range(chunks)]
+        gated = [keep.tile([P, j_tiles, N_GATE], F32, name=f"gated{h}") for h in range(M // N_GATE)]
+
+        def gather(t, a, b):
+            window = planes[t][:].indirect(offsets[:, a // LIST_ROWS : b // LIST_ROWS])
+            nc.vector.tensor_tensor(picked[0][:, t, a:b], window, weights[:, a:b], MULT)
+
+        def x_round(j):
+            h, c0 = divmod(j * J_TILE, G)
+            interleave(X_ON[j], x_bf[j][:], picked[h][:, :, c0 : c0 + J_TILE])
+
+        def x_quant(j):
+            nc.vector.quantize_mx(out=x_codes[j][:].bitcast(FP8X4), scales=x_scales[j][:], in_=x_bf[j][:])
+
+        def gate(j, h):
+            bank = psum.tile([P, N_GATE], F32, name="gate_bank")
+            nc.tensor.matmul_mx(
+                out=bank[:],
+                lhsT=x_codes[j][:].bitcast(FP8X4),
+                lhsT_scale=x_scales[j][:],
+                rhs=gate_words[:, 2 * h * N_GATE : 2 * (h + 1) * N_GATE].bitcast(FP4X4),
+                rhs_scale=gate_scales[:, h * N_GATE : (h + 1) * N_GATE],
+                start=True,
+                stop=True,
+            )
+            nc.scalar.activation(out=gated[h][:, j, :], in_=bank[:], func=SILU)
+
+        def w_round(c):
+            half = N_UP // 2
+            a, b = W_ON[2 * c], W_ON[2 * c + 1]
+            if a == b:
+                interleave(a, w_bf[c][:], w_raw[c][:])
+            else:
+                interleave(a, w_bf[c][:, : PACK * half], w_raw[c][:, :, :half])
+                interleave(b, w_bf[c][:, PACK * half :], w_raw[c][:, :, half:])
+
+        def w_quant(c):
+            nc.vector.quantize_mx(out=w_codes[c][:].bitcast(FP8X4), scales=w_scales[c][:], in_=w_bf[c][:])
+
+        def up(c, pair):
+            h, n0 = divmod(c * N_UP, N_GATE)
+            bank = psum.tile([P, 2, N_UP], F32, name="up_bank")
+            for u in range(2):
+                j = 2 * pair + u
+                nc.tensor.matmul_mx(
+                    out=bank[:, u, :],
+                    lhsT=x_codes[j][:].bitcast(FP8X4),
+                    lhsT_scale=x_scales[j][:],
+                    rhs=w_codes[c][:].bitcast(FP8X4),
+                    rhs_scale=w_scales[c][:],
+                    start=True,
+                    stop=True,
+                )
+            result = keep.tile([P, 2, N_UP], F32, name=f"result{c}_{pair}")
+            nc.vector.tensor_tensor(result[:], bank[:], gated[h][:, 2 * pair : 2 * pair + 2, n0 : n0 + N_UP], MULT)
+            rows = out[2 * pair * J_TILE : 2 * (pair + 1) * J_TILE, c * N_UP : (c + 1) * N_UP]
+            nc.sync.dma_start(out=rows.rearrange("(u p) n -> p u n", p=P), in_=result[:])
+
+        for t in range(PACK - 1):
+            gather(t, 0, S)
+        for j in range(j_tiles):
+            gather(PACK - 1, j * J_TILE, (j + 1) * J_TILE)
+        for j in range(j_tiles):
+            x_round(j)
+        x_quant(0)
+        gate(0, 0)
+        x_quant(1)
+        gate(1, 0)
+        w_round(0)
+        x_quant(2)
+        gate(2, 0)
+        w_quant(0)
+        x_quant(3)
+        gate(3, 0)
+        w_round(1)
+        up(0, 0)
+        w_quant(1)
+        up(0, 1)
+        w_round(2)
+        gate(0, 1)
+        gate(1, 1)
+        up(1, 0)
+        w_quant(2)
+        up(1, 1)
+        w_round(3)
+        gate(2, 1)
+        gate(3, 1)
+        up(2, 0)
+        w_quant(3)
+        up(3, 0)
+        up(2, 1)
+        up(3, 1)

@@ -23,8 +23,8 @@ J_TILE = 128
 N_GATE = 512
 N_UP = 256
 LIST_ROWS = 16
-X_ON = ["S","S","S","V"]
-W_ON = ["V","V","V","V","S","S","S","S"]
+X_ON = ["S","S","S","S"]
+W_ON = ["V","V","V","V","V","V","S","S"]
 
 
 def tile_list_hglu_tm_none_kernel(tc, xT, w4_words, w4_scales, w8, wgt, offs, out):
@@ -49,11 +49,15 @@ def tile_list_hglu_tm_none_kernel(tc, xT, w4_words, w4_scales, w8, wgt, offs, ou
         offsets = keep.tile([P, S // LIST_ROWS], U16, name="offsets")
         gate_scales = keep.tile([P, M], U8, name="gate_scales", align_bytes=64)
         nc.vector.memset(gate_scales[:].bitcast(I32), 0)
+        warm_in = keep.tile([P, 8], F32, name="warm_in")
+        warm_out = keep.tile([P, 8], F32, name="warm_out")
+        nc.gpsimd.memset(warm_in[:], 0.0)
+        nc.scalar.activation(out=warm_out[:], in_=warm_in[:], func=SILU)
 
         weights = keep.tile([P, S], F32, name="weights")
         planes = [keep.tile([P, T], F32, name=f"plane{t}") for t in range(PACK)]
         gate_words = keep.tile([P, 2 * M], U8, name="gate_words", align_bytes=64)
-        w_raw = [keep.tile([P, PACK, N_UP], F32, name=f"w_raw{c}") for c in range(chunks)]
+        w_raw = [keep.tile([P, PACK, N_UP], F32, name=f"w_raw{c}", tag=f"w_raw{c}", align_bytes=64) for c in range(chunks)]
         x_rows = xT.rearrange("(p t) n -> p t n", t=PACK)
         w_rows = w8.rearrange("(p t) n -> p t n", t=PACK)
 
@@ -64,6 +68,9 @@ def tile_list_hglu_tm_none_kernel(tc, xT, w4_words, w4_scales, w8, wgt, offs, ou
                 nc.sync.dma_start(out=weights[:], in_=wgt)
             elif name == "w4":
                 nc.sync.dma_start(out=gate_words[:].bitcast(I32), in_=w4_words[0].bitcast(I32))
+            elif name in ("wgtC", "wgtD"):
+                h = 0 if name == "wgtC" else 1
+                nc.sync.dma_start(out=weights[:, h * 256 : (h + 1) * 256], in_=wgt[:, h * 256 : (h + 1) * 256])
             elif name == "sc":
                 for q in range(4):
                     nc.sync.dma_start(out=gate_scales[32 * q : 32 * q + 4, :].bitcast(I32), in_=w4_scales[0, 4 * q : 4 * q + 4, :].bitcast(I32))
@@ -74,19 +81,19 @@ def tile_list_hglu_tm_none_kernel(tc, xT, w4_words, w4_scales, w8, wgt, offs, ou
                 c = int(name[1])
                 nc.sync.dma_start(out=w_raw[c][:], in_=w_rows[:, :, c * N_UP : (c + 1) * N_UP])
 
-        for name in ["offs","wgt","x0","sc","x1","x2","x3","w4","u0","u1","u2","u3"]:
+        for name in ["offs","wgt","x0","sc","x1","x2","x3","u0","w4","u1","u2","u3"]:
             ld(name)
 
         G = 512
         groups = S // G
         picked = [keep.tile([P, PACK, G], F32, name=f"picked{h}") for h in range(groups)]
         x_bf = [keep.tile([P, PACK * J_TILE], BF16, name=f"x_bf{j}", align_bytes=64) for j in range(j_tiles)]
-        x_codes = [keep.tile([P, J_TILE], U32, name=f"x_codes{j}", align_bytes=64) for j in range(j_tiles)]
+        x_codes = {}
         x_scales = [keep.tile([P, J_TILE], U8, name=f"x_scales{j}", align_bytes=64) for j in range(j_tiles)]
         w_bf = [keep.tile([P, PACK * N_UP], BF16, name=f"w_bf{c}", align_bytes=64) for c in range(chunks)]
-        w_codes = [keep.tile([P, N_UP], U32, name=f"w_codes{c}", align_bytes=64) for c in range(chunks)]
-        w_scales = [keep.tile([P, N_UP], U8, name=f"w_scales{c}", align_bytes=64) for c in range(chunks)]
-        gated = [keep.tile([P, j_tiles, N_GATE], F32, name=f"gated{h}") for h in range(M // N_GATE)]
+        w_codes = [keep.tile([P, N_GATE], U32, name=f"w_codes{h}", align_bytes=64) for h in range(2)]
+        w_scales = [keep.tile([P, N_GATE], U8, name=f"w_scales{h}", align_bytes=64) for h in range(2)]
+        gated = {}
 
         def gather(t, a, b):
             window = planes[t][:].indirect(offsets[:, a // LIST_ROWS : b // LIST_ROWS])
@@ -96,10 +103,11 @@ def tile_list_hglu_tm_none_kernel(tc, xT, w4_words, w4_scales, w8, wgt, offs, ou
             h, c0 = divmod(j * J_TILE, G)
             interleave(X_ON[j], x_bf[j][:], picked[h][:, :, c0 : c0 + J_TILE])
 
-        def x_quant(j):
+        def x_quant(j, tag=None):
+            x_codes[j] = keep.tile([P, J_TILE], U32, name=f"x_codes{j}", tag=tag or f"x_codes{j}", align_bytes=64)
             nc.vector.quantize_mx(out=x_codes[j][:].bitcast(FP8X4), scales=x_scales[j][:], in_=x_bf[j][:])
 
-        def gate(j, h):
+        def gate(j, h, tag=None):
             bank = psum.tile([P, N_GATE], F32, name="gate_bank")
             nc.tensor.matmul_mx(
                 out=bank[:],
@@ -110,7 +118,9 @@ def tile_list_hglu_tm_none_kernel(tc, xT, w4_words, w4_scales, w8, wgt, offs, ou
                 start=True,
                 stop=True,
             )
-            nc.scalar.activation(out=gated[h][:, j, :], in_=bank[:], func=SILU)
+            if j % 2 == 0:
+                gated[j // 2, h] = keep.tile([P, 2, N_GATE], F32, name=f"gated{j}_{h}", tag=tag or f"gated{j}_{h}", align_bytes=64)
+            nc.scalar.activation(out=gated[j // 2, h][:, j % 2, :], in_=bank[:], func=SILU)
 
         def w_round(c):
             half = N_UP // 2
@@ -122,9 +132,10 @@ def tile_list_hglu_tm_none_kernel(tc, xT, w4_words, w4_scales, w8, wgt, offs, ou
                 interleave(b, w_bf[c][:, PACK * half :], w_raw[c][:, :, half:])
 
         def w_quant(c):
-            nc.vector.quantize_mx(out=w_codes[c][:].bitcast(FP8X4), scales=w_scales[c][:], in_=w_bf[c][:])
+            h, n0 = divmod(c * N_UP, N_GATE)
+            nc.vector.quantize_mx(out=w_codes[h][:, n0 : n0 + N_UP].bitcast(FP8X4), scales=w_scales[h][:, n0 : n0 + N_UP], in_=w_bf[c][:])
 
-        def up(c, pair):
+        def up(c, pair, tag=None):
             h, n0 = divmod(c * N_UP, N_GATE)
             bank = psum.tile([P, 2, N_UP], F32, name="up_bank")
             for u in range(2):
@@ -133,47 +144,68 @@ def tile_list_hglu_tm_none_kernel(tc, xT, w4_words, w4_scales, w8, wgt, offs, ou
                     out=bank[:, u, :],
                     lhsT=x_codes[j][:].bitcast(FP8X4),
                     lhsT_scale=x_scales[j][:],
-                    rhs=w_codes[c][:].bitcast(FP8X4),
-                    rhs_scale=w_scales[c][:],
+                    rhs=w_codes[h][:, n0 : n0 + N_UP].bitcast(FP8X4),
+                    rhs_scale=w_scales[h][:, n0 : n0 + N_UP],
                     start=True,
                     stop=True,
                 )
-            result = keep.tile([P, 2, N_UP], F32, name=f"result{c}_{pair}")
-            nc.vector.tensor_tensor(result[:], bank[:], gated[h][:, 2 * pair : 2 * pair + 2, n0 : n0 + N_UP], MULT)
+            result = keep.tile([P, 2, N_UP], F32, name=f"result_p{c}_{pair}", tag=tag or f"result_p{c}_{pair}", align_bytes=64)
+            nc.vector.tensor_tensor(result[:], bank[:], gated[pair, h][:, :, n0 : n0 + N_UP], MULT)
             rows = out[2 * pair * J_TILE : 2 * (pair + 1) * J_TILE, c * N_UP : (c + 1) * N_UP]
             nc.sync.dma_start(out=rows.rearrange("(u p) n -> p u n", p=P), in_=result[:])
 
-        for t in range(PACK - 1):
-            gather(t, 0, S)
-        for j in range(j_tiles):
-            gather(PACK - 1, j * J_TILE, (j + 1) * J_TILE)
-        for j in range(j_tiles):
-            x_round(j)
+        def upj(j, h, tag=None, parts=1):
+            bank = psum.tile([P, N_GATE], F32, name="up_bank")
+            nc.tensor.matmul_mx(
+                out=bank[:],
+                lhsT=x_codes[j][:].bitcast(FP8X4),
+                lhsT_scale=x_scales[j][:],
+                rhs=w_codes[h][:].bitcast(FP8X4),
+                rhs_scale=w_scales[h][:],
+                start=True,
+                stop=True,
+            )
+            result = keep.tile([P, N_GATE], F32, name=f"result{j}_{h}", tag=tag or f"result{j}_{h}", align_bytes=64)
+            width = N_GATE // parts
+            for a in range(0, N_GATE, width):
+                nc.vector.tensor_tensor(result[:, a : a + width], bank[:, a : a + width], gated[j // 2, h][:, j % 2, a : a + width], MULT)
+                nc.sync.dma_start(out=out[j * J_TILE : (j + 1) * J_TILE, h * N_GATE + a : h * N_GATE + a + width], in_=result[:, a : a + width])
+
+        gather(0, 0, 512)
+        gather(1, 0, 512)
+        gather(2, 0, 512)
+        gather(3, 0, 128)
+        gather(3, 128, 256)
+        gather(3, 256, 512)
+        x_round(0)
+        x_round(1)
+        x_round(2)
+        x_round(3)
         x_quant(0)
-        gate(0, 0)
-        x_quant(1)
-        gate(1, 0)
         w_round(0)
-        x_quant(2)
-        gate(2, 0)
-        w_quant(0)
-        x_quant(3)
-        gate(3, 0)
+        x_quant(1)
         w_round(1)
-        up(0, 0)
+        w_quant(0)
+        x_quant(2)
         w_quant(1)
-        up(0, 1)
+        x_quant(3, "w_raw1")
+        gate(0, 0)
+        gate(1, 0)
+        gate(2, 0)
+        gate(3, 0)
         w_round(2)
+        w_quant(2)
+        w_round(3)
+        w_quant(3)
+        upj(0, 0)
+        upj(1, 0)
+        upj(2, 0)
+        upj(3, 0)
         gate(0, 1)
         gate(1, 1)
-        up(1, 0)
-        w_quant(2)
-        up(1, 1)
-        w_round(3)
-        gate(2, 1)
-        gate(3, 1)
+        gate(2, 1, "w_raw3")
+        gate(3, 1, "w_raw3")
         up(2, 0)
-        w_quant(3)
-        up(3, 0)
         up(2, 1)
+        up(3, 0)
         up(3, 1)

from contextlib import ExitStack

import concourse.mybir as mybir

K, M, T, S = 512, 1024, 1024, 512
FLOPS = 2 * 2 * K * M * S

F32 = mybir.dt.float32
BF16 = mybir.dt.bfloat16
I32 = mybir.dt.int32
U32 = mybir.dt.uint32
U16 = mybir.dt.uint16
U8 = mybir.dt.uint8
FP8X4 = mybir.dt.float8_e4m3fn_x4
FP4X4 = mybir.dt.float4_e2m1fn_x4
MULT = mybir.AluOpType.mult
ADD = mybir.AluOpType.add
SILU = mybir.ActivationFunctionType.Silu

P = 128
PACK = 4
J_TILE = 128
N_GATE = 512
N_UP = 256
LIST_ROWS = 16
X_ON = ["S","S","S","S"]
W_ON = ["V","V","V","V","V","V","S","S"]


def tile_list_hglu_tm_none_kernel(tc, xT, w4_words, w4_scales, w8, wgt, offs, out):
    nc = tc.nc
    j_tiles = S // J_TILE
    chunks = M // N_UP

    def interleave(engine, dst, src):
        d = dst.rearrange("p (c i t) -> p c t i", i=4, t=PACK)
        s = src.rearrange("p t (c i) -> p c t i", i=4)
        if engine == "S":
            nc.scalar.copy(out=d, in_=s)
        elif engine == "V":
            nc.vector.tensor_copy(out=d, in_=s)
        else:
            nc.gpsimd.tensor_scalar(out=d, in0=s, scalar1=1.0, scalar2=0.0, op0=MULT, op1=ADD)

    with ExitStack() as ctx:
        keep = ctx.enter_context(tc.tile_pool(name="keep", bufs=1))
        psum = ctx.enter_context(tc.psum_pool(name="psum", bufs=4))

        offsets = keep.tile([P, S // LIST_ROWS], U16, name="offsets")
        gate_scales = keep.tile([P, M], U8, name="gate_scales", align_bytes=64)
        nc.vector.memset(gate_scales[:].bitcast(I32), 0)
        warm_in = keep.tile([P, 8], F32, name="warm_in")
        warm_out = keep.tile([P, 8], F32, name="warm_out")
        nc.gpsimd.memset(warm_in[:], 0.0)
        nc.scalar.activation(out=warm_out[:], in_=warm_in[:], func=SILU)

        weights = keep.tile([P, S], F32, name="weights")
        planes = [keep.tile([P, T], F32, name=f"plane{t}") for t in range(PACK)]
        gate_words = keep.tile([P, 2 * M], U8, name="gate_words", align_bytes=64)
        w_raw = [keep.tile([P, PACK, N_UP], F32, name=f"w_raw{c}", tag=f"w_raw{c}", align_bytes=64) for c in range(chunks)]
        x_rows = xT.rearrange("(p t) n -> p t n", t=PACK)
        w_rows = w8.rearrange("(p t) n -> p t n", t=PACK)

        def ld(name):
            if name == "offs":
                nc.sync.dma_start(offsets[:], offs)
            elif name == "wgt":
                nc.sync.dma_start(out=weights[:], in_=wgt)
            elif name == "w4":
                nc.sync.dma_start(out=gate_words[:].bitcast(I32), in_=w4_words[0].bitcast(I32))
            elif name in ("wgtC", "wgtD"):
                h = 0 if name == "wgtC" else 1
                nc.sync.dma_start(out=weights[:, h * 256 : (h + 1) * 256], in_=wgt[:, h * 256 : (h + 1) * 256])
            elif name == "sc":
                for q in range(4):
                    nc.sync.dma_start(out=gate_scales[32 * q : 32 * q + 4, :].bitcast(I32), in_=w4_scales[0, 4 * q : 4 * q + 4, :].bitcast(I32))
            elif name[0] == "x":
                t = int(name[1])
                nc.sync.dma_start(out=planes[t][:], in_=x_rows[:, t, :])
            else:
                c = int(name[1])
                nc.sync.dma_start(out=w_raw[c][:], in_=w_rows[:, :, c * N_UP : (c + 1) * N_UP])

        for name in ["offs","wgt","x0","sc","x1","x2","x3","u0","w4","u1","u2","u3"]:
            ld(name)

        G = 512
        groups = S // G
        picked = [keep.tile([P, PACK, G], F32, name=f"picked{h}") for h in range(groups)]
        x_bf = [keep.tile([P, PACK * J_TILE], BF16, name=f"x_bf{j}", align_bytes=64) for j in range(j_tiles)]
        x_codes = {}
        x_scales = [keep.tile([P, J_TILE], U8, name=f"x_scales{j}", align_bytes=64) for j in range(j_tiles)]
        w_bf = [keep.tile([P, PACK * N_UP], BF16, name=f"w_bf{c}", align_bytes=64) for c in range(chunks)]
        w_codes = [keep.tile([P, N_GATE], U32, name=f"w_codes{h}", align_bytes=64) for h in range(2)]
        w_scales = [keep.tile([P, N_GATE], U8, name=f"w_scales{h}", align_bytes=64) for h in range(2)]
        gated = {}

        def gather(t, a, b):
            window = planes[t][:].indirect(offsets[:, a // LIST_ROWS : b // LIST_ROWS])
            nc.vector.tensor_tensor(picked[0][:, t, a:b], window, weights[:, a:b], MULT)

        def x_round(j):
            h, c0 = divmod(j * J_TILE, G)
            interleave(X_ON[j], x_bf[j][:], picked[h][:, :, c0 : c0 + J_TILE])

        def x_quant(j, tag=None):
            x_codes[j] = keep.tile([P, J_TILE], U32, name=f"x_codes{j}", tag=tag or f"x_codes{j}", align_bytes=64)
            nc.vector.quantize_mx(out=x_codes[j][:].bitcast(FP8X4), scales=x_scales[j][:], in_=x_bf[j][:])

        def gate(j, h, tag=None):
            bank = psum.tile([P, N_GATE], F32, name="gate_bank")
            nc.tensor.matmul_mx(
                out=bank[:],
                lhsT=x_codes[j][:].bitcast(FP8X4),
                lhsT_scale=x_scales[j][:],
                rhs=gate_words[:, 2 * h * N_GATE : 2 * (h + 1) * N_GATE].bitcast(FP4X4),
                rhs_scale=gate_scales[:, h * N_GATE : (h + 1) * N_GATE],
                start=True,
                stop=True,
            )
            if j % 2 == 0:
                gated[j // 2, h] = keep.tile([P, 2, N_GATE], F32, name=f"gated{j}_{h}", tag=tag or f"gated{j}_{h}", align_bytes=64)
            nc.scalar.activation(out=gated[j // 2, h][:, j % 2, :], in_=bank[:], func=SILU)

        def w_round(c):
            half = N_UP // 2
            a, b = W_ON[2 * c], W_ON[2 * c + 1]
            if a == b:
                interleave(a, w_bf[c][:], w_raw[c][:])
            else:
                interleave(a, w_bf[c][:, : PACK * half], w_raw[c][:, :, :half])
                interleave(b, w_bf[c][:, PACK * half :], w_raw[c][:, :, half:])

        def w_quant(c):
            h, n0 = divmod(c * N_UP, N_GATE)
            nc.vector.quantize_mx(out=w_codes[h][:, n0 : n0 + N_UP].bitcast(FP8X4), scales=w_scales[h][:, n0 : n0 + N_UP], in_=w_bf[c][:])

        def up(c, pair, tag=None):
            h, n0 = divmod(c * N_UP, N_GATE)
            bank = psum.tile([P, 2, N_UP], F32, name="up_bank")
            for u in range(2):
                j = 2 * pair + u
                nc.tensor.matmul_mx(
                    out=bank[:, u, :],
                    lhsT=x_codes[j][:].bitcast(FP8X4),
                    lhsT_scale=x_scales[j][:],
                    rhs=w_codes[h][:, n0 : n0 + N_UP].bitcast(FP8X4),
                    rhs_scale=w_scales[h][:, n0 : n0 + N_UP],
                    start=True,
                    stop=True,
                )
            result = keep.tile([P, 2, N_UP], F32, name=f"result_p{c}_{pair}", tag=tag or f"result_p{c}_{pair}", align_bytes=64)
            nc.vector.tensor_tensor(result[:], bank[:], gated[pair, h][:, :, n0 : n0 + N_UP], MULT)
            rows = out[2 * pair * J_TILE : 2 * (pair + 1) * J_TILE, c * N_UP : (c + 1) * N_UP]
            nc.sync.dma_start(out=rows.rearrange("(u p) n -> p u n", p=P), in_=result[:])

        def upj(j, h, tag=None, parts=1):
            bank = psum.tile([P, N_GATE], F32, name="up_bank")
            nc.tensor.matmul_mx(
                out=bank[:],
                lhsT=x_codes[j][:].bitcast(FP8X4),
                lhsT_scale=x_scales[j][:],
                rhs=w_codes[h][:].bitcast(FP8X4),
                rhs_scale=w_scales[h][:],
                start=True,
                stop=True,
            )
            result = keep.tile([P, N_GATE], F32, name=f"result{j}_{h}", tag=tag or f"result{j}_{h}", align_bytes=64)
            width = N_GATE // parts
            for a in range(0, N_GATE, width):
                nc.vector.tensor_tensor(result[:, a : a + width], bank[:, a : a + width], gated[j // 2, h][:, j % 2, a : a + width], MULT)
                nc.sync.dma_start(out=out[j * J_TILE : (j + 1) * J_TILE, h * N_GATE + a : h * N_GATE + a + width], in_=result[:, a : a + width])

        gather(0, 0, 512)
        gather(1, 0, 512)
        gather(2, 0, 512)
        gather(3, 0, 128)
        gather(3, 128, 256)
        gather(3, 256, 512)
        x_round(0)
        x_round(1)
        x_round(2)
        x_round(3)
        x_quant(0)
        w_round(0)
        x_quant(1)
        w_round(1)
        w_quant(0)
        x_quant(2)
        w_quant(1)
        x_quant(3, "w_raw1")
        gate(0, 0)
        gate(1, 0)
        gate(2, 0)
        gate(3, 0)
        w_round(2)
        w_quant(2)
        w_round(3)
        w_quant(3)
        upj(0, 0)
        upj(1, 0)
        upj(2, 0)
        upj(3, 0)
        gate(0, 1)
        gate(1, 1)
        gate(2, 1, "w_raw3")
        gate(3, 1, "w_raw3")
        up(2, 0)
        up(2, 1)
        up(3, 0)
        up(3, 1)
